import numpy as np
import ml_dtypes


def mxq(x, axis, fmt="e4m3"):
    dtype, down = {"e4m3": (ml_dtypes.float8_e4m3fn, 7), "e5m2": (ml_dtypes.float8_e5m2, 14)}[fmt]
    v = np.moveaxis(np.asarray(x, np.float32).astype(ml_dtypes.bfloat16).astype(np.float64), axis, -1)
    blocks = v.reshape(v.shape[:-1] + (-1, 32))
    amax = np.abs(blocks).max(-1, keepdims=True)
    byte = np.maximum(np.where(amax > 0, np.frexp(amax)[1] - 1 + 127, 0) - down, 1)
    scale = np.exp2(byte - 127.0)
    codes = (blocks / scale).astype(np.float32).astype(dtype).astype(np.float64)
    return np.moveaxis((codes * scale).reshape(v.shape), -1, axis)


WIDE = False


def mx_kscale(k):
    if not WIDE:
        return np.ones(k)
    levels = np.array([10, -10, 5, -5, 0])
    if k % 512:
        return np.exp2(np.random.permutation(np.resize(levels, k // 32))).repeat(32)
    a = np.empty((k // 512, 16))
    for p in range(k // 512):
        a[p, :8] = np.random.permutation(np.resize(levels, 8))
        for g in range(8):
            far = levels[np.abs(levels - a[p, g]) >= 10]
            a[p, g + 8] = far[np.random.randint(len(far))]
    return np.exp2(a.ravel()).repeat(32)


def f64(x):
    return np.asarray(x).astype(np.float64)


def striped(idx):
    return np.tile(idx.reshape(-1, 16).T, (8, 1)).astype(np.uint16)


def unstriped(offs):
    return offs[:16].T.reshape(-1).astype(np.int64)


def striped8(idx):
    return np.concatenate([x.reshape(-1, 16).T for x in idx]).astype(np.uint16)


def runs(offs, k):
    lists = np.stack([offs[16 * r : 16 * r + 16].T.reshape(-1) for r in range(8)]).astype(np.int64)
    return lists[np.arange(k) % 512 // 64]


def pack_weight(w):
    k, n = w.shape
    w = f64(np.asarray(w, np.float32).astype(ml_dtypes.bfloat16)).reshape(k // 32, 32, n)
    amax = np.abs(w).max(1)
    byte = np.clip(np.where(amax > 0, np.frexp(amax)[1] - 1 + 127 - 7, 1), 1, 254)
    scaled = (w * np.exp2(127.0 - byte)[:, None, :]).reshape(k, n).astype(np.float32)
    words = np.ascontiguousarray(scaled.reshape(k // 512, 128, 4, n).transpose(0, 1, 3, 2)).astype(ml_dtypes.float8_e4m3fn).view(np.uint8)
    return words, np.ascontiguousarray(byte.astype(np.uint8).reshape(k // 512, 16, n))


def unpack_weight(words, scales):
    g, p, n, _ = words.shape
    vals = np.ascontiguousarray(words).view(ml_dtypes.float8_e4m3fn).astype(np.float64) * np.repeat(np.exp2(scales.astype(np.float64) - 127.0), 8, axis=1)[..., None]
    return vals.transpose(0, 1, 3, 2).reshape(g * 512, n)


def relu(v):
    return np.maximum(v, 0.0)

def planes(y):
    n, m = y.shape
    v = y.astype(np.float32).astype(ml_dtypes.bfloat16).astype(np.float64).reshape(n // 32, 32, m)
    top = np.abs(v).max(1)
    byte = np.clip(np.where(top > 0, np.frexp(top)[1] - 1 + 127 - 7, 1), 1, 254)
    codes = (v * np.exp2(127.0 - byte)[:, None, :]).reshape(n, m).astype(np.float32).astype(ml_dtypes.float8_e4m3fn).view(np.uint8)
    words = codes.reshape(n // 512, 128, 4, m).transpose(0, 1, 3, 2)
    return np.ascontiguousarray(words), np.ascontiguousarray(byte.astype(np.uint8).reshape(n // 512, 16, m))


K, T, S, V, G, H = 512, 2048, 1024, 512, 2048, 512


def setup_inputs():
    n = np.random.standard_normal
    s = mx_kscale(K)[:, None]
    packed_xT = pack_weight(n((K, T)) * s)
    packed_dT = pack_weight(n((K, G)) / s)
    return {
        "x_words": packed_xT[0],
        "x_scales": packed_xT[1],
        "d_words": packed_dT[0],
        "d_scales": packed_dT[1],
        "gs": (np.random.uniform(0.5, 1.5, (K, 1)) * s).astype(np.float32),
        "offs": striped(np.random.permutation(T)[:S]),
        "k1": striped8(np.random.randint(0, G, (8, H))),
        "l1": striped8(np.stack([np.random.permutation(S)[:V] for _ in range(8)])),
        "r1": striped8(np.stack([np.random.permutation(S)[:V] for _ in range(8)])),
        "k2": striped8(np.random.randint(0, G, (8, H))),
        "k3": striped8(np.random.randint(0, G, (8, H))),
    }


def reference(x_words, x_scales, d_words, d_scales, gs, offs, k1, l1, r1, k2, k3):
    d_k2 = unpack_weight(d_words, d_scales)[np.arange(K)[:, None], runs(k2, K)]
    d_k1 = unpack_weight(d_words, d_scales)[np.arange(K)[:, None], runs(k1, K)]
    xq = unpack_weight(x_words, x_scales)[:, unstriped(offs)]
    h = relu(0.0625 * (d_k1.T @ xq))
    z = f64(gs) * (h[np.arange(H)[:, None], runs(l1, H)])
    d_k3 = unpack_weight(d_words, d_scales)[np.arange(K)[:, None], runs(k3, K)]
    z2 = f64(gs) * (h[np.arange(H)[:, None], runs(r1, H)])
    out_0 = 0.0625 * ((d_k2.T @ mxq(z, 0, "e4m3")) + (d_k3.T @ mxq(z2, 0, "e4m3")))
    return (out_0,) + planes(out_0)

@@ -1,0 +1,204 @@
+from contextlib import ExitStack
+
+import concourse.mybir as mybir
+
+F32 = mybir.dt.float32
+BF16 = mybir.dt.bfloat16
+I32 = mybir.dt.int32
+U32 = mybir.dt.uint32
+U16 = mybir.dt.uint16
+U8 = mybir.dt.uint8
+FP8X4 = mybir.dt.float8_e4m3fn_x4
+ACT = mybir.ActivationFunctionType
+ALU = mybir.AluOpType
+
+P = 128
+PACK = 4
+K, T, S, V, G, H = 512, 2048, 1024, 512, 2048, 512
+SH = S // 2
+VH = V // 2
+FLOPS = 2 * K * H * S + 2 * 2 * K * H * V
+
+
+def tile_picked_pqtree_relu_po_kernel(
+    tc, x_words, x_scales, d_words, d_scales, gs, offs, k1, l1, r1, k2, k3, out_0, out_1, out_2
+):
+    nc = tc.nc
+    with ExitStack() as ctx:
+        keep = ctx.enter_context(tc.tile_pool(name="keep", bufs=1))
+        psum = ctx.enter_context(tc.psum_pool(name="psum", bufs=1))
+
+        def sb(name, shape, dtype):
+            return keep.tile(shape, dtype, name=name, align_bytes=64)
+
+        def load_list(name, src):
+            t = keep.tile(list(src.shape), U16, name=name)
+            nc.sync.dma_start(t[:], src)
+            return t
+
+        def as_words(ap):
+            return ap.rearrange("p n t -> p (n t)").bitcast(I32)
+
+        ds_win = sb("ds_win", [P, G], U8)
+        xs_win = sb("xs_win", [P, T], U8)
+        nc.vector.memset(ds_win[:].bitcast(I32), 0)
+        nc.gpsimd.memset(xs_win[:].bitcast(I32), 0)
+
+        k1_t = load_list("k1_t", k1)
+        for j in range(2):
+            nc.sync.dma_start(ds_win[j:P:16, :].bitcast(I32), d_scales[0][j:16:2, :].bitcast(I32))
+        offs_t = load_list("offs_t", offs)
+        for q in range(4):
+            nc.sync.dma_start(xs_win[32 * q : 32 * q + 4, :].bitcast(I32), x_scales[0][4 * q : 4 * q + 4, :].bitcast(I32))
+        dw_win = sb("dw_win", [P, G], I32)
+        nc.sync.dma_start(dw_win[:], as_words(d_words[0]))
+        xw_win = sb("xw_win", [P, T], I32)
+        nc.sync.dma_start(xw_win[:], as_words(x_words[0]))
+        gs_t = sb("gs_t", [P, PACK], F32)
+        nc.sync.dma_start(gs_t[:], gs.rearrange("(p t) o -> p (t o)", t=PACK))
+        k2_t = load_list("k2_t", k2)
+        k3_t = load_list("k3_t", k3)
+        l1_t = load_list("l1_t", l1)
+        r1_t = load_list("r1_t", r1)
+
+        gs16 = sb("gs16", [P, PACK], F32)
+        nc.scalar.activation(gs16[:], gs_t[:], ACT.Copy, scale=0.0625)
+
+        def deal(dst, src):
+            nc.vector.tensor_copy(dst.rearrange("p (a t m) -> p a m t", t=PACK, m=P), src.rearrange("p (a m t) -> p a m t", t=PACK, m=P))
+
+        def pick_scales(name, lists, queue):
+            n = len(lists)
+            got = sb(name + "_sg", [P, n * H], U8)
+            for a, lst in enumerate(lists):
+                nc.vector.tensor_copy(got[:, a * H : (a + 1) * H], ds_win[:].indirect(lst[:]))
+            dealt = sb(name + "_sd", [P, n * H], U8)
+            deal(dealt[:], got[:])
+            for j in range(2):
+                queue.dma_start(dealt[2 + j : P : 32, :].bitcast(I32), dealt[16 + j : P : 32, :].bitcast(I32))
+            return dealt
+
+        def pick_words(name, lists):
+            n = len(lists)
+            got = sb(name + "_wg", [P, n * H], I32)
+            for a, lst in enumerate(lists):
+                nc.vector.tensor_copy(got[:, a * H : (a + 1) * H].bitcast(U32), dw_win[:].bitcast(U32).indirect(lst[:]))
+            dealt = sb(name + "_wd", [P, n * H], I32)
+            deal(dealt[:], got[:])
+            return dealt
+
+        w1_s = pick_scales("w1", [k1_t], nc.scalar)
+        x_s = sb("x_s", [P, S], U8)
+        nc.vector.tensor_copy(x_s[:], xs_win[:].indirect(offs_t[:]))
+        w1_w = pick_words("w1", [k1_t])
+
+        h = [sb("h%d" % t, [P, S], F32) for t in range(PACK)]
+
+        def weigh(u, t, pos):
+            nc.scalar.activation(h[t][:, u * SH : (u + 1) * SH], pos[:], ACT.Copy, scale=gs16[:, t : t + 1])
+
+        waiting = []
+        for u in range(2):
+            x_w = sb("x_w%d" % u, [P, SH], I32)
+            nc.vector.tensor_copy(x_w[:].bitcast(U32), xw_win[:].bitcast(U32).indirect(offs_t[:, u * SH // 16 : (u + 1) * SH // 16]))
+            for t in range(PACK):
+                acc = psum.tile([P, SH], F32, name="acc", tag="bank%d" % (PACK * u + t))
+                cols = slice(t * P, (t + 1) * P)
+                nc.tensor.matmul_mx(
+                    out=acc[:], lhsT=w1_w[:, cols].bitcast(FP8X4), lhsT_scale=w1_s[:, cols],
+                    rhs=x_w[:].bitcast(FP8X4), rhs_scale=x_s[:, u * SH : (u + 1) * SH], start=True, stop=True,
+                )
+                pos = sb("pos%d%d" % (u, t), [P, SH], F32)
+                nc.scalar.activation(pos[:], acc[:], ACT.Relu)
+                if waiting:
+                    weigh(*waiting.pop())
+                waiting.append((u, t, pos))
+        weigh(*waiting.pop())
+
+        w23_s = pick_scales("w23", [k2_t, k3_t], nc.sync)
+        w23_w = pick_words("w23", [k2_t, k3_t])
+
+        y_words = sb("y_words", [P, V], I32)
+        y_scales = sb("y_scales", [P, V], U8)
+        out_rows = out_0.rearrange("(p t) v -> p t v", t=PACK)
+        out_words = as_words(out_1[0])
+        children = [l1_t, r1_t]
+
+        def fetch(u, a, t, planes):
+            nc.vector.tensor_copy(planes[:, t * VH : (t + 1) * VH], h[t][:].indirect(children[a][:, u * VH // 16 : (u + 1) * VH // 16]))
+
+        def weave(woven, planes, split):
+            src = planes.rearrange("p (t v) -> p v t", t=PACK)
+            dst = woven.rearrange("p (v t) -> p v t", t=PACK)
+            if split > 0:
+                nc.vector.tensor_copy(dst[:, :split, :], src[:, :split, :])
+            if split < VH:
+                nc.scalar.copy(dst[:, split:, :], src[:, split:, :])
+
+        def quantise(woven, words, scales):
+            nc.vector.quantize_mx(out=words.bitcast(FP8X4), scales=scales, in_=woven)
+
+        def product(u, a, woven, accs):
+            z_w = sb("z_w%d%d" % (u, a), [P, VH], I32)
+            z_s = sb("z_s%d%d" % (u, a), [P, VH], U8)
+            quantise(woven, z_w[:], z_s[:])
+            for t in range(PACK):
+                cols = slice(a * H + t * P, a * H + (t + 1) * P)
+                nc.tensor.matmul_mx(
+                    out=accs[t][:], lhsT=w23_w[:, cols].bitcast(FP8X4), lhsT_scale=w23_s[:, cols],
+                    rhs=z_w[:].bitcast(FP8X4), rhs_scale=z_s[:], start=(a == 0), stop=(a == 1),
+                )
+
+        def finish(u, accs, last):
+            vcols = slice(u * VH, (u + 1) * VH)
+            y = sb("y%d" % u, [P, PACK * VH], F32)
+            for t in range(PACK):
+                dst = y[:, t * VH : (t + 1) * VH]
+                if last and t % 2 == 1:
+                    nc.vector.tensor_scalar(dst, accs[t][:], 0.0625, None, ALU.mult)
+                else:
+                    nc.scalar.activation(dst, accs[t][:], ACT.Copy, scale=0.0625)
+            nc.sync.dma_start(out_rows[:, :, vcols], y[:].rearrange("p (t v) -> p t v", t=PACK))
+            return y
+
+        def hand_on(u, y, split):
+            vcols = slice(u * VH, (u + 1) * VH)
+            woven = sb("y_woven%d" % u, [P, PACK * VH], BF16)
+            weave(woven[:], y[:], split)
+            quantise(woven[:], y_words[:, vcols], y_scales[:, vcols])
+            nc.sync.dma_start(out_words[:, vcols], y_words[:, vcols])
+
+        W = PACK * VH
+        planes00 = sb("planes00", [P, W], BF16)
+        planes01 = sb("planes01", [P, W], BF16)
+        lane_a = sb("lane_a", [P, W + W // 2], BF16)
+        lane_b = sb("lane_b", [P, 2 * W], BF16)
+        lane_c = sb("lane_c", [P, W], BF16)
+        planes10, z00 = lane_a[:, :W], lane_a[:, W // 2 :]
+        z01, planes11, z10 = lane_b[:, :W], lane_b[:, W // 2 : W + W // 2], lane_b[:, W:]
+        accs = [[psum.tile([P, VH], F32, name="acc", tag="bank%d" % (PACK * u + t)) for t in range(PACK)] for u in range(2)]
+
+        for t in range(PACK):
+            fetch(0, 0, t, planes00[:])
+            fetch(0, 1, t, planes01[:])
+        weave(z00, planes00[:], 0)
+        weave(z01, planes01[:], 0)
+        for t in range(PACK):
+            if t == 2:
+                product(0, 0, z00, accs[0])
+            fetch(1, 0, t, planes10)
+        weave(z10, planes10, 0)
+        product(0, 1, z01, accs[0])
+        y0 = finish(0, accs[0], False)
+        for t in range(PACK):
+            if t == 2:
+                product(1, 0, z10, accs[1])
+            fetch(1, 1, t, planes11)
+        weave(lane_c[:], planes11, 160)
+        product(1, 1, lane_c[:], accs[1])
+        hand_on(0, y0, VH)
+        y1 = finish(1, accs[1], True)
+        hand_on(1, y1, 160)
+        for q in range(4):
+            eng = nc.scalar if q % 2 else nc.sync
+            eng.dma_start(out_2[0][4 * q : 4 * q + 4, :].bitcast(I32), y_scales[32 * q : 32 * q + 4, :].bitcast(I32))

@@ -26,6 +26,7 @@ def tile_picked_pqtree_relu_po_kernel(
     nc = tc.nc
     with ExitStack() as ctx:
         keep = ctx.enter_context(tc.tile_pool(name="keep", bufs=1))
+        reuse = ctx.enter_context(tc.tile_pool(name="reuse", bufs=1))
         psum = ctx.enter_context(tc.psum_pool(name="psum", bufs=1))
 
         def sb(name, shape, dtype):
@@ -45,78 +46,86 @@ def tile_picked_pqtree_relu_po_kernel(
         nc.gpsimd.memset(xs_win[:].bitcast(I32), 0)
 
         k1_t = load_list("k1_t", k1)
+        offs_t = load_list("offs_t", offs)
+        k2_t = load_list("k2_t", k2)
+        r1_t = load_list("r1_t", r1)
+        gs_t = sb("gs_t", [P, PACK], F32)
+        nc.sync.dma_start(gs_t[:], gs.rearrange("(p t) o -> p (t o)", t=PACK))
         for j in range(2):
             nc.sync.dma_start(ds_win[j:P:16, :].bitcast(I32), d_scales[0][j:16:2, :].bitcast(I32))
-        offs_t = load_list("offs_t", offs)
+        xw_win = sb("xw_win", [P, T], I32)
+        nc.sync.dma_start(xw_win[:], as_words(x_words[0]))
         for q in range(4):
             nc.sync.dma_start(xs_win[32 * q : 32 * q + 4, :].bitcast(I32), x_scales[0][4 * q : 4 * q + 4, :].bitcast(I32))
         dw_win = sb("dw_win", [P, G], I32)
         nc.sync.dma_start(dw_win[:], as_words(d_words[0]))
-        xw_win = sb("xw_win", [P, T], I32)
-        nc.sync.dma_start(xw_win[:], as_words(x_words[0]))
-        gs_t = sb("gs_t", [P, PACK], F32)
-        nc.sync.dma_start(gs_t[:], gs.rearrange("(p t) o -> p (t o)", t=PACK))
-        k2_t = load_list("k2_t", k2)
-        k3_t = load_list("k3_t", k3)
         l1_t = load_list("l1_t", l1)
-        r1_t = load_list("r1_t", r1)
+        k3_t = load_list("k3_t", k3)
 
         gs16 = sb("gs16", [P, PACK], F32)
         nc.scalar.activation(gs16[:], gs_t[:], ACT.Copy, scale=0.0625)
 
-        def deal(dst, src):
-            nc.vector.tensor_copy(dst.rearrange("p (a t m) -> p a m t", t=PACK, m=P), src.rearrange("p (a m t) -> p a m t", t=PACK, m=P))
+        def deal(dst, src, line):
+            nc.vector.tensor_copy(
+                dst.rearrange("p (a t c i) -> p a c t i", t=PACK, c=P // line, i=line),
+                src.rearrange("p (a c i t) -> p a c t i", t=PACK, c=P // line, i=line),
+            )
 
-        def pick_scales(name, lists, queue):
-            n = len(lists)
-            got = sb(name + "_sg", [P, n * H], U8)
-            for a, lst in enumerate(lists):
-                nc.vector.tensor_copy(got[:, a * H : (a + 1) * H], ds_win[:].indirect(lst[:]))
-            dealt = sb(name + "_sd", [P, n * H], U8)
-            deal(dealt[:], got[:])
-            for j in range(2):
-                queue.dma_start(dealt[2 + j : P : 32, :].bitcast(I32), dealt[16 + j : P : 32, :].bitcast(I32))
-            return dealt
+        def pick_scales(got, lst):
+            nc.vector.tensor_copy(got[:], ds_win[:].indirect(lst[:]))
+            return got
 
-        def pick_words(name, lists):
-            n = len(lists)
-            got = sb(name + "_wg", [P, n * H], I32)
-            for a, lst in enumerate(lists):
-                nc.vector.tensor_copy(got[:, a * H : (a + 1) * H].bitcast(U32), dw_win[:].bitcast(U32).indirect(lst[:]))
-            dealt = sb(name + "_wd", [P, n * H], I32)
-            deal(dealt[:], got[:])
-            return dealt
+        def pick_words(got, lst):
+            nc.vector.tensor_copy(got.bitcast(U32), dw_win[:].bitcast(U32).indirect(lst[:]))
 
-        w1_s = pick_scales("w1", [k1_t], nc.scalar)
-        x_s = sb("x_s", [P, S], U8)
-        nc.vector.tensor_copy(x_s[:], xs_win[:].indirect(offs_t[:]))
-        w1_w = pick_words("w1", [k1_t])
-
+        w1_got = pick_scales(sb("w1_got", [P, H], U8), k1_t)
+        w1_s = sb("w1_s", [P, H], U8)
+        deal(w1_s[:], w1_got[:], 16)
+        for j in range(2):
+            nc.scalar.dma_start(w1_s[2 + j : P : 32, :].bitcast(I32), w1_s[16 + j : P : 32, :].bitcast(I32))
+        w2_got = pick_scales(sb("w2_got", [P, H], U8), k2_t)
         h = [sb("h%d" % t, [P, S], F32) for t in range(PACK)]
-
-        def weigh(u, t, pos):
-            nc.scalar.activation(h[t][:, u * SH : (u + 1) * SH], pos[:], ACT.Copy, scale=gs16[:, t : t + 1])
-
-        waiting = []
+        W = PACK * VH
+        lane = sb("lane", [P, W + S], F32)
+        planes01, planes10, planes11 = lane[:, :W], lane[:, W : 2 * W], lane[:, VH : W + VH]
+        pos = [sb("pos%d" % t, [P, S], F32) for t in range(PACK - 1)] + [lane[:, W:]]
         for u in range(2):
-            x_w = sb("x_w%d" % u, [P, SH], I32)
-            nc.vector.tensor_copy(x_w[:].bitcast(U32), xw_win[:].bitcast(U32).indirect(offs_t[:, u * SH // 16 : (u + 1) * SH // 16]))
+            leaves = offs_t[:, u * SH // 16 : (u + 1) * SH // 16]
+            if u == 0:
+                x_s = sb("x_s0", [P, SH], U8)
+                x_w = sb("x_w0", [P, SH], I32)
+            else:
+                x_s = reuse.tile([P, SH], U8, name="x_s1", offset=4160, align_bytes=64)
+                x_w = reuse.tile([P, SH], I32, name="x_w1", offset=5696, align_bytes=64)
+            nc.vector.tensor_copy(x_w[:].bitcast(U32), xw_win[:].bitcast(U32).indirect(leaves))
+            nc.vector.tensor_copy(x_s[:], xs_win[:].indirect(leaves))
+            if u == 0:
+                w1_wg = reuse.tile([P, H], I32, name="w1_wg", offset=4096, align_bytes=64)
+                pick_words(w1_wg[:], k1_t)
+                w1_w = sb("w1_w", [P, H], I32)
+                deal(w1_w[:], w1_wg[:], 4)
             for t in range(PACK):
                 acc = psum.tile([P, SH], F32, name="acc", tag="bank%d" % (PACK * u + t))
                 cols = slice(t * P, (t + 1) * P)
                 nc.tensor.matmul_mx(
                     out=acc[:], lhsT=w1_w[:, cols].bitcast(FP8X4), lhsT_scale=w1_s[:, cols],
-                    rhs=x_w[:].bitcast(FP8X4), rhs_scale=x_s[:, u * SH : (u + 1) * SH], start=True, stop=True,
+                    rhs=x_w[:].bitcast(FP8X4), rhs_scale=x_s[:], start=True, stop=True,
                 )
-                pos = sb("pos%d%d" % (u, t), [P, SH], F32)
-                nc.scalar.activation(pos[:], acc[:], ACT.Relu)
-                if waiting:
-                    weigh(*waiting.pop())
-                waiting.append((u, t, pos))
-        weigh(*waiting.pop())
+                nc.scalar.activation(pos[t][:, u * SH : (u + 1) * SH], acc[:], ACT.Relu)
+                if u == 1:
+                    nc.scalar.activation(h[t][:], pos[t][:, :], ACT.Copy, scale=gs16[:, t : t + 1])
 
-        w23_s = pick_scales("w23", [k2_t, k3_t], nc.sync)
-        w23_w = pick_words("w23", [k2_t, k3_t])
+        w23_got = reuse.tile([P, 2 * H], I32, name="w23_got", offset=64, align_bytes=64)
+        w23_w = sb("w23_w", [P, 2 * H], I32)
+        for a, lst in enumerate([k2_t, k3_t]):
+            pick_words(w23_got[:, a * H : (a + 1) * H], lst)
+        w3_got = pick_scales(reuse.tile([P, H], U8, name="w3_got", offset=4672, align_bytes=64), k3_t)
+        deal(w23_w[:], w23_got[:], 4)
+        packed = reuse.tile([P, H], U8, name="packed", offset=5184, align_bytes=64)
+        nc.gpsimd.memset(packed[:].bitcast(I32), 0)
+        for a, got in enumerate([w2_got, w3_got]):
+            for row, src in enumerate([0, 1, 16, 17]):
+                nc.sync.dma_start(packed[4 * a + row : P : 32, :].bitcast(I32), got[src:P:32, :].bitcast(I32))
 
         y_words = sb("y_words", [P, V], I32)
         y_scales = sb("y_scales", [P, V], U8)
@@ -128,26 +137,29 @@ def tile_picked_pqtree_relu_po_kernel(
             nc.vector.tensor_copy(planes[:, t * VH : (t + 1) * VH], h[t][:].indirect(children[a][:, u * VH // 16 : (u + 1) * VH // 16]))
 
         def weave(woven, planes, split):
-            src = planes.rearrange("p (t v) -> p v t", t=PACK)
-            dst = woven.rearrange("p (v t) -> p v t", t=PACK)
+            src = planes.rearrange("p (t c i) -> p c t i", t=PACK, i=4)
+            dst = woven.rearrange("p (c i t) -> p c t i", t=PACK, i=4)
             if split > 0:
-                nc.vector.tensor_copy(dst[:, :split, :], src[:, :split, :])
+                nc.vector.tensor_copy(dst[:, : split // 4], src[:, : split // 4])
             if split < VH:
-                nc.scalar.copy(dst[:, split:, :], src[:, split:, :])
+                nc.scalar.copy(dst[:, split // 4 :], src[:, split // 4 :])
 
         def quantise(woven, words, scales):
             nc.vector.quantize_mx(out=words.bitcast(FP8X4), scales=scales, in_=woven)
 
-        def product(u, a, woven, accs):
-            z_w = sb("z_w%d%d" % (u, a), [P, VH], I32)
-            z_s = sb("z_s%d%d" % (u, a), [P, VH], U8)
+        def products(name, sides, woven, accs):
+            z_w = sb(name + "_w", [P, len(sides) * VH], I32)
+            z_s = sb(name + "_s", [P, len(sides) * VH], U8)
             quantise(woven, z_w[:], z_s[:])
             for t in range(PACK):
-                cols = slice(a * H + t * P, a * H + (t + 1) * P)
-                nc.tensor.matmul_mx(
-                    out=accs[t][:], lhsT=w23_w[:, cols].bitcast(FP8X4), lhsT_scale=w23_s[:, cols],
-                    rhs=z_w[:].bitcast(FP8X4), rhs_scale=z_s[:], start=(a == 0), stop=(a == 1),
-                )
+                for n, a in enumerate(sides):
+                    zcols = slice(n * VH, (n + 1) * VH)
+                    nc.tensor.matmul_mx(
+                        out=accs[t][:],
+                        lhsT=w23_w[:, a * H + t * P : a * H + (t + 1) * P].bitcast(FP8X4),
+                        lhsT_scale=w23_s[4 * a : P, t * P : (t + 1) * P],
+                        rhs=z_w[:, zcols].bitcast(FP8X4), rhs_scale=z_s[:, zcols], start=(a == 0), stop=(a == 1),
+                    )
 
         def finish(u, accs, last):
             vcols = slice(u * VH, (u + 1) * VH)
@@ -161,44 +173,42 @@ def tile_picked_pqtree_relu_po_kernel(
             nc.sync.dma_start(out_rows[:, :, vcols], y[:].rearrange("p (t v) -> p t v", t=PACK))
             return y
 
-        def hand_on(u, y, split):
+        def hand_on(u, woven):
             vcols = slice(u * VH, (u + 1) * VH)
-            woven = sb("y_woven%d" % u, [P, PACK * VH], BF16)
-            weave(woven[:], y[:], split)
             quantise(woven[:], y_words[:, vcols], y_scales[:, vcols])
             nc.sync.dma_start(out_words[:, vcols], y_words[:, vcols])
 
-        W = PACK * VH
-        planes00 = sb("planes00", [P, W], BF16)
-        planes01 = sb("planes01", [P, W], BF16)
-        lane_a = sb("lane_a", [P, W + W // 2], BF16)
-        lane_b = sb("lane_b", [P, 2 * W], BF16)
-        lane_c = sb("lane_c", [P, W], BF16)
-        planes10, z00 = lane_a[:, :W], lane_a[:, W // 2 :]
-        z01, planes11, z10 = lane_b[:, :W], lane_b[:, W // 2 : W + W // 2], lane_b[:, W:]
+        planes00 = sb("planes00", [P, W], F32)
+        z0 = sb("z0", [P, 2 * W], BF16)
+        z10 = sb("z10", [P, W], BF16)
+        z11 = sb("z11", [P, W], BF16)
+        y_woven = [sb("y_woven%d" % u, [P, W], BF16) for u in range(2)]
         accs = [[psum.tile([P, VH], F32, name="acc", tag="bank%d" % (PACK * u + t)) for t in range(PACK)] for u in range(2)]
 
         for t in range(PACK):
             fetch(0, 0, t, planes00[:])
-            fetch(0, 1, t, planes01[:])
-        weave(z00, planes00[:], 0)
-        weave(z01, planes01[:], 0)
-        for t in range(PACK):
+            fetch(0, 1, t, planes01)
             if t == 2:
-                product(0, 0, z00, accs[0])
+                w23_s = keep.tile([P, H], U8, name="w23_s", tag="pos2", align_bytes=64)
+                deal(w23_s[:], packed[:], 16)
+        weave(z0[:, :W], planes00[:], 0)
+        weave(z0[:, W:], planes01, 0)
+        for t in range(PACK):
             fetch(1, 0, t, planes10)
-        weave(z10, planes10, 0)
-        product(0, 1, z01, accs[0])
+        weave(z10[:], planes10, 0)
+        products("z0", [0, 1], z0[:], accs[0])
         y0 = finish(0, accs[0], False)
         for t in range(PACK):
-            if t == 2:
-                product(1, 0, z10, accs[1])
+            if t == 3:
+                products("z10", [0], z10[:], accs[1])
             fetch(1, 1, t, planes11)
-        weave(lane_c[:], planes11, 160)
-        product(1, 1, lane_c[:], accs[1])
-        hand_on(0, y0, VH)
+        weave(z11[:], planes11, 160)
+        weave(y_woven[0][:], y0[:], 128)
+        products("z11", [1], z11[:], accs[1])
         y1 = finish(1, accs[1], True)
-        hand_on(1, y1, 160)
+        weave(y_woven[1][:], y1[:], 160)
+        hand_on(0, y_woven[0])
+        hand_on(1, y_woven[1])
         for q in range(4):
             eng = nc.scalar if q % 2 else nc.sync
             eng.dma_start(out_2[0][4 * q : 4 * q + 4, :].bitcast(I32), y_scales[32 * q : 32 * q + 4, :].bitcast(I32))

@@ -14,9 +14,22 @@ ALU = mybir.AluOpType
 
 P = 128
 PACK = 4
+QUADS = 4
+GROUP = 16
 K, T, S, V, G, H = 512, 2048, 1024, 512, 2048, 512
 SH = S // 2
 VH = V // 2
+W = PACK * VH
+SIXTEENTH = 0.0625
+LINE_WORDS, LINE_BYTES = 4, 16
+ALIGN = 64
+VECTOR_SHARE_LAST, VECTOR_SHARE_FIRST = 160, 128
+AT_W1_WG = 2 * H * 4
+AT_W23_GOT = ALIGN
+AT_X_S1 = AT_W1_WG + ALIGN
+AT_W3_GOT = AT_X_S1 + SH
+AT_PACKED = AT_W3_GOT + H
+AT_X_W1 = AT_PACKED + H
 FLOPS = 2 * K * H * S + 2 * 2 * K * H * V
 
 
@@ -30,12 +43,15 @@ def tile_picked_pqtree_relu_po_kernel(
         psum = ctx.enter_context(tc.psum_pool(name="psum", bufs=1))
 
         def sb(name, shape, dtype):
-            return keep.tile(shape, dtype, name=name, align_bytes=64)
+            return keep.tile(shape, dtype, name=name, align_bytes=ALIGN)
+
+        def placed(name, shape, dtype, offset):
+            return reuse.tile(shape, dtype, name=name, offset=offset, align_bytes=ALIGN)
 
         def load_list(name, src):
-            t = keep.tile(list(src.shape), U16, name=name)
-            nc.sync.dma_start(t[:], src)
-            return t
+            tile = keep.tile(list(src.shape), U16, name=name)
+            nc.sync.dma_start(tile[:], src)
+            return tile
 
         def as_words(ap):
             return ap.rearrange("p n t -> p (n t)").bitcast(I32)
@@ -52,18 +68,18 @@ def tile_picked_pqtree_relu_po_kernel(
         gs_t = sb("gs_t", [P, PACK], F32)
         nc.sync.dma_start(gs_t[:], gs.rearrange("(p t) o -> p (t o)", t=PACK))
         for j in range(2):
-            nc.sync.dma_start(ds_win[j:P:16, :].bitcast(I32), d_scales[0][j:16:2, :].bitcast(I32))
+            nc.sync.dma_start(ds_win[j:P:GROUP, :].bitcast(I32), d_scales[0][j:16:2, :].bitcast(I32))
+        l1_t = load_list("l1_t", l1)
         xw_win = sb("xw_win", [P, T], I32)
         nc.sync.dma_start(xw_win[:], as_words(x_words[0]))
-        for q in range(4):
+        for q in range(QUADS):
             nc.sync.dma_start(xs_win[32 * q : 32 * q + 4, :].bitcast(I32), x_scales[0][4 * q : 4 * q + 4, :].bitcast(I32))
         dw_win = sb("dw_win", [P, G], I32)
         nc.sync.dma_start(dw_win[:], as_words(d_words[0]))
-        l1_t = load_list("l1_t", l1)
         k3_t = load_list("k3_t", k3)
 
         gs16 = sb("gs16", [P, PACK], F32)
-        nc.scalar.activation(gs16[:], gs_t[:], ACT.Copy, scale=0.0625)
+        nc.scalar.activation(gs16[:], gs_t[:], ACT.Copy, scale=SIXTEENTH)
 
         def deal(dst, src, line):
             nc.vector.tensor_copy(
@@ -71,39 +87,40 @@ def tile_picked_pqtree_relu_po_kernel(
                 src.rearrange("p (a c i t) -> p a c t i", t=PACK, c=P // line, i=line),
             )
 
-        def pick_scales(got, lst):
-            nc.vector.tensor_copy(got[:], ds_win[:].indirect(lst[:]))
+        def pick_scales(got, codes):
+            nc.vector.tensor_copy(got[:], ds_win[:].indirect(codes[:]))
             return got
 
-        def pick_words(got, lst):
-            nc.vector.tensor_copy(got.bitcast(U32), dw_win[:].bitcast(U32).indirect(lst[:]))
+        def pick_words(got, codes):
+            nc.vector.tensor_copy(got.bitcast(U32), dw_win[:].bitcast(U32).indirect(codes[:]))
 
         w1_got = pick_scales(sb("w1_got", [P, H], U8), k1_t)
         w1_s = sb("w1_s", [P, H], U8)
-        deal(w1_s[:], w1_got[:], 16)
+        deal(w1_s[:], w1_got[:], LINE_BYTES)
         for j in range(2):
-            nc.scalar.dma_start(w1_s[2 + j : P : 32, :].bitcast(I32), w1_s[16 + j : P : 32, :].bitcast(I32))
+            nc.scalar.dma_start(w1_s[2 + j : P : 32, :].bitcast(I32), w1_s[GROUP + j : P : 32, :].bitcast(I32))
         w2_got = pick_scales(sb("w2_got", [P, H], U8), k2_t)
+
         h = [sb("h%d" % t, [P, S], F32) for t in range(PACK)]
-        W = PACK * VH
         lane = sb("lane", [P, W + S], F32)
         planes01, planes10, planes11 = lane[:, :W], lane[:, W : 2 * W], lane[:, VH : W + VH]
         pos = [sb("pos%d" % t, [P, S], F32) for t in range(PACK - 1)] + [lane[:, W:]]
+
         for u in range(2):
-            leaves = offs_t[:, u * SH // 16 : (u + 1) * SH // 16]
+            leaves = offs_t[:, u * SH // GROUP : (u + 1) * SH // GROUP]
             if u == 0:
                 x_s = sb("x_s0", [P, SH], U8)
                 x_w = sb("x_w0", [P, SH], I32)
             else:
-                x_s = reuse.tile([P, SH], U8, name="x_s1", offset=4160, align_bytes=64)
-                x_w = reuse.tile([P, SH], I32, name="x_w1", offset=5696, align_bytes=64)
+                x_s = placed("x_s1", [P, SH], U8, AT_X_S1)
+                x_w = placed("x_w1", [P, SH], I32, AT_X_W1)
             nc.vector.tensor_copy(x_w[:].bitcast(U32), xw_win[:].bitcast(U32).indirect(leaves))
             nc.vector.tensor_copy(x_s[:], xs_win[:].indirect(leaves))
             if u == 0:
-                w1_wg = reuse.tile([P, H], I32, name="w1_wg", offset=4096, align_bytes=64)
+                w1_wg = placed("w1_wg", [P, H], I32, AT_W1_WG)
                 pick_words(w1_wg[:], k1_t)
                 w1_w = sb("w1_w", [P, H], I32)
-                deal(w1_w[:], w1_wg[:], 4)
+                deal(w1_w[:], w1_wg[:], LINE_WORDS)
             for t in range(PACK):
                 acc = psum.tile([P, SH], F32, name="acc", tag="bank%d" % (PACK * u + t))
                 cols = slice(t * P, (t + 1) * P)
@@ -115,17 +132,17 @@ def tile_picked_pqtree_relu_po_kernel(
                 if u == 1:
                     nc.scalar.activation(h[t][:], pos[t][:, :], ACT.Copy, scale=gs16[:, t : t + 1])
 
-        w23_got = reuse.tile([P, 2 * H], I32, name="w23_got", offset=64, align_bytes=64)
+        w23_got = placed("w23_got", [P, 2 * H], I32, AT_W23_GOT)
         w23_w = sb("w23_w", [P, 2 * H], I32)
-        for a, lst in enumerate([k2_t, k3_t]):
-            pick_words(w23_got[:, a * H : (a + 1) * H], lst)
-        w3_got = pick_scales(reuse.tile([P, H], U8, name="w3_got", offset=4672, align_bytes=64), k3_t)
-        deal(w23_w[:], w23_got[:], 4)
-        packed = reuse.tile([P, H], U8, name="packed", offset=5184, align_bytes=64)
+        for a, codes in enumerate([k2_t, k3_t]):
+            pick_words(w23_got[:, a * H : (a + 1) * H], codes)
+        w3_got = pick_scales(placed("w3_got", [P, H], U8, AT_W3_GOT), k3_t)
+        deal(w23_w[:], w23_got[:], LINE_WORDS)
+        packed = placed("packed", [P, H], U8, AT_PACKED)
         nc.gpsimd.memset(packed[:].bitcast(I32), 0)
         for a, got in enumerate([w2_got, w3_got]):
-            for row, src in enumerate([0, 1, 16, 17]):
-                nc.sync.dma_start(packed[4 * a + row : P : 32, :].bitcast(I32), got[src:P:32, :].bitcast(I32))
+            for row, src_row in enumerate([0, 1, GROUP, GROUP + 1]):
+                nc.sync.dma_start(packed[4 * a + row : P : 32, :].bitcast(I32), got[src_row:P:32, :].bitcast(I32))
 
         y_words = sb("y_words", [P, V], I32)
         y_scales = sb("y_scales", [P, V], U8)
@@ -134,20 +151,21 @@ def tile_picked_pqtree_relu_po_kernel(
         children = [l1_t, r1_t]
 
         def fetch(u, a, t, planes):
-            nc.vector.tensor_copy(planes[:, t * VH : (t + 1) * VH], h[t][:].indirect(children[a][:, u * VH // 16 : (u + 1) * VH // 16]))
+            entries = children[a][:, u * VH // GROUP : (u + 1) * VH // GROUP]
+            nc.vector.tensor_copy(planes[:, t * VH : (t + 1) * VH], h[t][:].indirect(entries))
 
-        def weave(woven, planes, split):
-            src = planes.rearrange("p (t c i) -> p c t i", t=PACK, i=4)
-            dst = woven.rearrange("p (c i t) -> p c t i", t=PACK, i=4)
-            if split > 0:
-                nc.vector.tensor_copy(dst[:, : split // 4], src[:, : split // 4])
-            if split < VH:
-                nc.scalar.copy(dst[:, split // 4 :], src[:, split // 4 :])
+        def weave(woven, planes, vector_cols):
+            src = planes.rearrange("p (t c i) -> p c t i", t=PACK, i=LINE_WORDS)
+            dst = woven.rearrange("p (c i t) -> p c t i", t=PACK, i=LINE_WORDS)
+            cut = vector_cols // LINE_WORDS
+            if cut > 0:
+                nc.vector.tensor_copy(dst[:, :cut], src[:, :cut])
+            nc.scalar.copy(dst[:, cut:], src[:, cut:])
 
         def quantise(woven, words, scales):
             nc.vector.quantize_mx(out=words.bitcast(FP8X4), scales=scales, in_=woven)
 
-        def products(name, sides, woven, accs):
+        def products(name, sides, woven, banks):
             z_w = sb(name + "_w", [P, len(sides) * VH], I32)
             z_s = sb(name + "_s", [P, len(sides) * VH], U8)
             quantise(woven, z_w[:], z_s[:])
@@ -155,22 +173,21 @@ def tile_picked_pqtree_relu_po_kernel(
                 for n, a in enumerate(sides):
                     zcols = slice(n * VH, (n + 1) * VH)
                     nc.tensor.matmul_mx(
-                        out=accs[t][:],
+                        out=banks[t][:],
                         lhsT=w23_w[:, a * H + t * P : a * H + (t + 1) * P].bitcast(FP8X4),
                         lhsT_scale=w23_s[4 * a : P, t * P : (t + 1) * P],
                         rhs=z_w[:, zcols].bitcast(FP8X4), rhs_scale=z_s[:, zcols], start=(a == 0), stop=(a == 1),
                     )
 
-        def finish(u, accs, last):
-            vcols = slice(u * VH, (u + 1) * VH)
-            y = sb("y%d" % u, [P, PACK * VH], F32)
+        def finish(u, banks):
+            y = sb("y%d" % u, [P, W], F32)
             for t in range(PACK):
                 dst = y[:, t * VH : (t + 1) * VH]
-                if last and t % 2 == 1:
-                    nc.vector.tensor_scalar(dst, accs[t][:], 0.0625, None, ALU.mult)
+                if u == 1 and t % 2 == 1:
+                    nc.vector.tensor_scalar(dst, banks[t][:], SIXTEENTH, None, ALU.mult)
                 else:
-                    nc.scalar.activation(dst, accs[t][:], ACT.Copy, scale=0.0625)
-            nc.sync.dma_start(out_rows[:, :, vcols], y[:].rearrange("p (t v) -> p t v", t=PACK))
+                    nc.scalar.activation(dst, banks[t][:], ACT.Copy, scale=SIXTEENTH)
+            nc.sync.dma_start(out_rows[:, :, u * VH : (u + 1) * VH], y[:].rearrange("p (t v) -> p t v", t=PACK))
             return y
 
         def hand_on(u, woven):
@@ -183,32 +200,34 @@ def tile_picked_pqtree_relu_po_kernel(
         z10 = sb("z10", [P, W], BF16)
         z11 = sb("z11", [P, W], BF16)
         y_woven = [sb("y_woven%d" % u, [P, W], BF16) for u in range(2)]
-        accs = [[psum.tile([P, VH], F32, name="acc", tag="bank%d" % (PACK * u + t)) for t in range(PACK)] for u in range(2)]
+        sums = [[psum.tile([P, VH], F32, name="acc", tag="bank%d" % (PACK * u + t)) for t in range(PACK)] for u in range(2)]
 
         for t in range(PACK):
             fetch(0, 0, t, planes00[:])
             fetch(0, 1, t, planes01)
-            if t == 2:
-                w23_s = keep.tile([P, H], U8, name="w23_s", tag="pos2", align_bytes=64)
-                deal(w23_s[:], packed[:], 16)
+            if t == PACK - 2:
+                w23_s = keep.tile([P, H], U8, name="w23_s", tag="pos%d" % t, align_bytes=ALIGN)
+                deal(w23_s[:], packed[:], LINE_BYTES)
         weave(z0[:, :W], planes00[:], 0)
         weave(z0[:, W:], planes01, 0)
+
         for t in range(PACK):
             fetch(1, 0, t, planes10)
         weave(z10[:], planes10, 0)
-        products("z0", [0, 1], z0[:], accs[0])
-        y0 = finish(0, accs[0], False)
+        products("z0", [0, 1], z0[:], sums[0])
+        y0 = finish(0, sums[0])
         for t in range(PACK):
-            if t == 3:
-                products("z10", [0], z10[:], accs[1])
+            if t == PACK - 1:
+                products("z10", [0], z10[:], sums[1])
             fetch(1, 1, t, planes11)
-        weave(z11[:], planes11, 160)
-        weave(y_woven[0][:], y0[:], 128)
-        products("z11", [1], z11[:], accs[1])
-        y1 = finish(1, accs[1], True)
-        weave(y_woven[1][:], y1[:], 160)
+
+        weave(z11[:], planes11, VECTOR_SHARE_LAST)
+        weave(y_woven[0][:], y0[:], VECTOR_SHARE_FIRST)
+        products("z11", [1], z11[:], sums[1])
+        y1 = finish(1, sums[1])
+        weave(y_woven[1][:], y1[:], VECTOR_SHARE_LAST)
         hand_on(0, y_woven[0])
         hand_on(1, y_woven[1])
-        for q in range(4):
-            eng = nc.scalar if q % 2 else nc.sync
-            eng.dma_start(out_2[0][4 * q : 4 * q + 4, :].bitcast(I32), y_scales[32 * q : 32 * q + 4, :].bitcast(I32))
+        for q in range(QUADS):
+            queue = nc.scalar if q % 2 else nc.sync
+            queue.dma_start(out_2[0][4 * q : 4 * q + 4, :].bitcast(I32), y_scales[32 * q : 32 * q + 4, :].bitcast(I32))

from contextlib import ExitStack

import concourse.mybir as mybir

F32 = mybir.dt.float32
BF16 = mybir.dt.bfloat16
I32 = mybir.dt.int32
U32 = mybir.dt.uint32
U16 = mybir.dt.uint16
U8 = mybir.dt.uint8
FP8X4 = mybir.dt.float8_e4m3fn_x4
ACT = mybir.ActivationFunctionType
ALU = mybir.AluOpType

P = 128
PACK = 4
QUADS = 4
GROUP = 16
K, T, S, V, G, H = 512, 2048, 1024, 512, 2048, 512
SH = S // 2
VH = V // 2
W = PACK * VH
SIXTEENTH = 0.0625
LINE_WORDS, LINE_BYTES = 4, 16
ALIGN = 64
VECTOR_SHARE_LAST, VECTOR_SHARE_FIRST = 160, 128
AT_W1_WG = 2 * H * 4
AT_W23_GOT = ALIGN
AT_X_S1 = AT_W1_WG + ALIGN
AT_W3_GOT = AT_X_S1 + SH
AT_PACKED = AT_W3_GOT + H
AT_X_W1 = AT_PACKED + H
FLOPS = 2 * K * H * S + 2 * 2 * K * H * V


def tile_picked_pqtree_relu_po_kernel(
    tc, x_words, x_scales, d_words, d_scales, gs, offs, k1, l1, r1, k2, k3, out_0, out_1, out_2
):
    nc = tc.nc
    with ExitStack() as ctx:
        keep = ctx.enter_context(tc.tile_pool(name="keep", bufs=1))
        reuse = ctx.enter_context(tc.tile_pool(name="reuse", bufs=1))
        psum = ctx.enter_context(tc.psum_pool(name="psum", bufs=1))

        def sb(name, shape, dtype):
            return keep.tile(shape, dtype, name=name, align_bytes=ALIGN)

        def placed(name, shape, dtype, offset):
            return reuse.tile(shape, dtype, name=name, offset=offset, align_bytes=ALIGN)

        def load_list(name, src):
            tile = keep.tile(list(src.shape), U16, name=name)
            nc.sync.dma_start(tile[:], src)
            return tile

        def as_words(ap):
            return ap.rearrange("p n t -> p (n t)").bitcast(I32)

        ds_win = sb("ds_win", [P, G], U8)
        xs_win = sb("xs_win", [P, T], U8)
        nc.vector.memset(ds_win[:].bitcast(I32), 0)
        nc.gpsimd.memset(xs_win[:].bitcast(I32), 0)

        k1_t = load_list("k1_t", k1)
        offs_t = load_list("offs_t", offs)
        k2_t = load_list("k2_t", k2)
        r1_t = load_list("r1_t", r1)
        gs_t = sb("gs_t", [P, PACK], F32)
        nc.sync.dma_start(gs_t[:], gs.rearrange("(p t) o -> p (t o)", t=PACK))
        for j in range(2):
            nc.sync.dma_start(ds_win[j:P:GROUP, :].bitcast(I32), d_scales[0][j:16:2, :].bitcast(I32))
        l1_t = load_list("l1_t", l1)
        xw_win = sb("xw_win", [P, T], I32)
        nc.sync.dma_start(xw_win[:], as_words(x_words[0]))
        for q in range(QUADS):
            nc.sync.dma_start(xs_win[32 * q : 32 * q + 4, :].bitcast(I32), x_scales[0][4 * q : 4 * q + 4, :].bitcast(I32))
        dw_win = sb("dw_win", [P, G], I32)
        nc.sync.dma_start(dw_win[:], as_words(d_words[0]))
        k3_t = load_list("k3_t", k3)

        gs16 = sb("gs16", [P, PACK], F32)
        nc.scalar.activation(gs16[:], gs_t[:], ACT.Copy, scale=SIXTEENTH)

        def deal(dst, src, line):
            nc.vector.tensor_copy(
                dst.rearrange("p (a t c i) -> p a c t i", t=PACK, c=P // line, i=line),
                src.rearrange("p (a c i t) -> p a c t i", t=PACK, c=P // line, i=line),
            )

        def pick_scales(got, codes):
            nc.vector.tensor_copy(got[:], ds_win[:].indirect(codes[:]))
            return got

        def pick_words(got, codes):
            nc.vector.tensor_copy(got.bitcast(U32), dw_win[:].bitcast(U32).indirect(codes[:]))

        w1_got = pick_scales(sb("w1_got", [P, H], U8), k1_t)
        w1_s = sb("w1_s", [P, H], U8)
        deal(w1_s[:], w1_got[:], LINE_BYTES)
        for j in range(2):
            nc.scalar.dma_start(w1_s[2 + j : P : 32, :].bitcast(I32), w1_s[GROUP + j : P : 32, :].bitcast(I32))
        w2_got = pick_scales(sb("w2_got", [P, H], U8), k2_t)

        h = [sb("h%d" % t, [P, S], F32) for t in range(PACK)]
        lane = sb("lane", [P, W + S], F32)
        planes01, planes10, planes11 = lane[:, :W], lane[:, W : 2 * W], lane[:, VH : W + VH]
        pos = [sb("pos%d" % t, [P, S], F32) for t in range(PACK - 1)] + [lane[:, W:]]

        for u in range(2):
            leaves = offs_t[:, u * SH // GROUP : (u + 1) * SH // GROUP]
            if u == 0:
                x_s = sb("x_s0", [P, SH], U8)
                x_w = sb("x_w0", [P, SH], I32)
            else:
                x_s = placed("x_s1", [P, SH], U8, AT_X_S1)
                x_w = placed("x_w1", [P, SH], I32, AT_X_W1)
            nc.vector.tensor_copy(x_w[:].bitcast(U32), xw_win[:].bitcast(U32).indirect(leaves))
            nc.vector.tensor_copy(x_s[:], xs_win[:].indirect(leaves))
            if u == 0:
                w1_wg = placed("w1_wg", [P, H], I32, AT_W1_WG)
                pick_words(w1_wg[:], k1_t)
                w1_w = sb("w1_w", [P, H], I32)
                deal(w1_w[:], w1_wg[:], LINE_WORDS)
            for t in range(PACK):
                acc = psum.tile([P, SH], F32, name="acc", tag="bank%d" % (PACK * u + t))
                cols = slice(t * P, (t + 1) * P)
                nc.tensor.matmul_mx(
                    out=acc[:], lhsT=w1_w[:, cols].bitcast(FP8X4), lhsT_scale=w1_s[:, cols],
                    rhs=x_w[:].bitcast(FP8X4), rhs_scale=x_s[:], start=True, stop=True,
                )
                nc.scalar.activation(pos[t][:, u * SH : (u + 1) * SH], acc[:], ACT.Relu)
                if u == 1:
                    nc.scalar.activation(h[t][:], pos[t][:, :], ACT.Copy, scale=gs16[:, t : t + 1])

        w23_got = placed("w23_got", [P, 2 * H], I32, AT_W23_GOT)
        w23_w = sb("w23_w", [P, 2 * H], I32)
        for a, codes in enumerate([k2_t, k3_t]):
            pick_words(w23_got[:, a * H : (a + 1) * H], codes)
        w3_got = pick_scales(placed("w3_got", [P, H], U8, AT_W3_GOT), k3_t)
        deal(w23_w[:], w23_got[:], LINE_WORDS)
        packed = placed("packed", [P, H], U8, AT_PACKED)
        nc.gpsimd.memset(packed[:].bitcast(I32), 0)
        for a, got in enumerate([w2_got, w3_got]):
            for row, src_row in enumerate([0, 1, GROUP, GROUP + 1]):
                nc.sync.dma_start(packed[4 * a + row : P : 32, :].bitcast(I32), got[src_row:P:32, :].bitcast(I32))

        y_words = sb("y_words", [P, V], I32)
        y_scales = sb("y_scales", [P, V], U8)
        out_rows = out_0.rearrange("(p t) v -> p t v", t=PACK)
        out_words = as_words(out_1[0])
        children = [l1_t, r1_t]

        def fetch(u, a, t, planes):
            entries = children[a][:, u * VH // GROUP : (u + 1) * VH // GROUP]
            nc.vector.tensor_copy(planes[:, t * VH : (t + 1) * VH], h[t][:].indirect(entries))

        def weave(woven, planes, vector_cols):
            src = planes.rearrange("p (t c i) -> p c t i", t=PACK, i=LINE_WORDS)
            dst = woven.rearrange("p (c i t) -> p c t i", t=PACK, i=LINE_WORDS)
            cut = vector_cols // LINE_WORDS
            if cut > 0:
                nc.vector.tensor_copy(dst[:, :cut], src[:, :cut])
            nc.scalar.copy(dst[:, cut:], src[:, cut:])

        def quantise(woven, words, scales):
            nc.vector.quantize_mx(out=words.bitcast(FP8X4), scales=scales, in_=woven)

        def products(name, sides, woven, banks):
            z_w = sb(name + "_w", [P, len(sides) * VH], I32)
            z_s = sb(name + "_s", [P, len(sides) * VH], U8)
            quantise(woven, z_w[:], z_s[:])
            for t in range(PACK):
                for n, a in enumerate(sides):
                    zcols = slice(n * VH, (n + 1) * VH)
                    nc.tensor.matmul_mx(
                        out=banks[t][:],
                        lhsT=w23_w[:, a * H + t * P : a * H + (t + 1) * P].bitcast(FP8X4),
                        lhsT_scale=w23_s[4 * a : P, t * P : (t + 1) * P],
                        rhs=z_w[:, zcols].bitcast(FP8X4), rhs_scale=z_s[:, zcols], start=(a == 0), stop=(a == 1),
                    )

        def finish(u, banks):
            y = sb("y%d" % u, [P, W], F32)
            for t in range(PACK):
                dst = y[:, t * VH : (t + 1) * VH]
                if u == 1 and t % 2 == 1:
                    nc.vector.tensor_scalar(dst, banks[t][:], SIXTEENTH, None, ALU.mult)
                else:
                    nc.scalar.activation(dst, banks[t][:], ACT.Copy, scale=SIXTEENTH)
            nc.sync.dma_start(out_rows[:, :, u * VH : (u + 1) * VH], y[:].rearrange("p (t v) -> p t v", t=PACK))
            return y

        def hand_on(u, woven):
            vcols = slice(u * VH, (u + 1) * VH)
            quantise(woven[:], y_words[:, vcols], y_scales[:, vcols])
            nc.sync.dma_start(out_words[:, vcols], y_words[:, vcols])

        planes00 = sb("planes00", [P, W], F32)
        z0 = sb("z0", [P, 2 * W], BF16)
        z10 = sb("z10", [P, W], BF16)
        z11 = sb("z11", [P, W], BF16)
        y_woven = [sb("y_woven%d" % u, [P, W], BF16) for u in range(2)]
        sums = [[psum.tile([P, VH], F32, name="acc", tag="bank%d" % (PACK * u + t)) for t in range(PACK)] for u in range(2)]

        for t in range(PACK):
            fetch(0, 0, t, planes00[:])
            fetch(0, 1, t, planes01)
            if t == PACK - 2:
                w23_s = keep.tile([P, H], U8, name="w23_s", tag="pos%d" % t, align_bytes=ALIGN)
                deal(w23_s[:], packed[:], LINE_BYTES)
        weave(z0[:, :W], planes00[:], 0)
        weave(z0[:, W:], planes01, 0)

        for t in range(PACK):
            fetch(1, 0, t, planes10)
        weave(z10[:], planes10, 0)
        products("z0", [0, 1], z0[:], sums[0])
        y0 = finish(0, sums[0])
        for t in range(PACK):
            if t == PACK - 1:
                products("z10", [0], z10[:], sums[1])
            fetch(1, 1, t, planes11)

        weave(z11[:], planes11, VECTOR_SHARE_LAST)
        weave(y_woven[0][:], y0[:], VECTOR_SHARE_FIRST)
        products("z11", [1], z11[:], sums[1])
        y1 = finish(1, sums[1])
        weave(y_woven[1][:], y1[:], VECTOR_SHARE_LAST)
        hand_on(0, y_woven[0])
        hand_on(1, y_woven[1])
        for q in range(QUADS):
            queue = nc.scalar if q % 2 else nc.sync
            queue.dma_start(out_2[0][4 * q : 4 * q + 4, :].bitcast(I32), y_scales[32 * q : 32 * q + 4, :].bitcast(I32))
